import numpy as np, ml_dtypes
CORES = [49,52,55,57,60,63,65,68,71,73,76,79]
N = 12
C = 256
def setup_inputs(rng):
    u = np.triu(np.ones((128, 128), np.float32)).astype(ml_dtypes.bfloat16)
    return {"x": rng.standard_normal((N, 128, C), dtype=np.float32).astype(ml_dtypes.bfloat16), "u": np.broadcast_to(u, (N, 128, 128)).copy()}
def setup_inputs_big(rng):
    d = setup_inputs(rng)
    for k in ("x", "u"): d[k] = (d[k].astype(np.float32) * 1024.0).astype(d[k].dtype)
    return d
def setup_inputs_small(rng):
    d = setup_inputs(rng)
    for k in ("x", "u"): d[k] = (d[k].astype(np.float32) * (1 / 1024.0)).astype(d[k].dtype)
    return d
def setup_inputs_apart(rng):
    d = setup_inputs(rng)
    f = (10.0 ** rng.permutation(np.linspace(-1.5, 1.5, N))).astype(np.float32).reshape(N, 1, 1)
    for k in ("x",): d[k] = (d[k].astype(np.float32) * f).astype(d[k].dtype)
    return d
def reference(x, u):
    X, U = x.astype(np.float64), u.astype(np.float64)
    y = np.zeros((N, 128, C)); c = np.zeros(C)
    for r in range(N):
        y[r] = U[r].T @ X[r] + c
        c = c + X[r].sum(axis=0)
    return {"y": y.astype(ml_dtypes.bfloat16)}

@@ -1,0 +1,130 @@
+from concourse.bass import DstId, RemoteDMATransfer
+
+SCRATCH = {
+    "xs": ("sbuf", [128, 256], "bfloat16"),
+    "us": ("sbuf", [128, 128], "bfloat16"),
+    "ones": ("sbuf", [128, 128], "bfloat16"),
+    "srow": ("sbuf", [128, 256], "bfloat16"),
+    "rows": ("sbuf", [128, 256], "bfloat16"),
+    "ys": ("sbuf", [128, 256], "bfloat16"),
+    "mine": ("dram", [128, 2], "bfloat16"),
+    "slots": ("dram", [12, 128, 2], "bfloat16"),
+    "py": ("psum", [128, 512], "float32"),
+    "ps": ("psum", [128, 512], "float32"),
+}
+SEMAPHORES = ["ones", "xin", "uin", "smm", "scp", "mined", "near", "far", "rin", "ymm", "ycp", "yout", "sent"]
+
+
+def rank_program(g, core, T, topo):
+    rank = T.rank_of(core)
+    if rank is None:
+        return
+    sem = T.sem
+    cores = list(T.cores)
+    n = len(cores)
+
+    chips = []
+    for c in cores:
+        if topo.chip(c) not in chips:
+            chips.append(topo.chip(c))
+    group = [[r for r in range(n) if topo.chip(cores[r]) == ch] for ch in chips]
+    kof = {}
+    for k, grp in enumerate(group):
+        assert grp == list(range(grp[0], grp[0] + len(grp)))
+        for r in grp:
+            kof[r] = k
+
+    def later(k):
+        return [r for grp in group[k + 1:] for r in grp]
+
+    relay = []
+    for k, grp in enumerate(group):
+        able = [r for r in grp if all(topo.may_write(cores[r], cores[d]) for d in later(k))]
+        relay.append(able[-1] if later(k) else None)
+
+    def near_order(d):
+        grp = group[kof[d]]
+        return [r for r in grp if r < d] + [r for r in grp if r > d]
+
+    def near_slot(d, q):
+        return 2 * kof[d] + near_order(d).index(q)
+
+    def near_dsts(q):
+        k = kof[q]
+        first = [relay[k]] if relay[k] is not None and relay[k] != q else []
+        return first + [d for d in group[k] if d > q and d not in first]
+
+    def engine(dsts, i):
+        m = topo.mask(core, cores[dsts[0]])
+        for d in dsts:
+            m &= topo.mask(core, cores[d])
+        bits = [1 << b for b in range(m.bit_length()) if (m >> b) & 1]
+        return bits[i % len(bits)]
+
+    def transfer(srcs, dsts, slot_of, eng, rsem):
+        ids = []
+        for d in dsts:
+            rid, pid, _se = topo.addr(cores[d])
+            ids.append(DstId(rid=rid, pnc=pid))
+        return RemoteDMATransfer(dst_ids=ids, dma_engine_mask=eng, remote_sem=rsem, srcs=srcs,
+                                 dsts=[T.slots[slot_of(d)] for d in dsts], alu_op=1 if len(srcs) > 1 else 0)
+
+    k = kof[rank]
+    m = 2 * k + len([r for r in group[k] if r < rank])
+    am_relay = relay[k] == rank
+    sends = am_relay or len(near_dsts(rank)) > 0
+    n_near = len([q for q in group[k] if q != rank and rank in near_dsts(q)])
+    n_far = 2 * k
+
+    g.sync.dma_start(T.xs[:], T.x[:]).then_inc(sem.xin, 16)
+    g.sync.dma_start(T.us[:], T.u[:]).then_inc(sem.uin, 16)
+
+    g.vector.memset(T.ones[:], 1.0).then_inc(sem.ones, 1)
+    if sends:
+        g.vector.wait_ge(sem.smm, 1)
+        g.vector.tensor_copy(T.srow[0:1, :], T.ps[0:1, 0:256]).then_inc(sem.scp, 1)
+
+    g.tensor.wait_ge(sem.ones, 1)
+    g.tensor.wait_ge(sem.xin, 16)
+    if sends:
+        g.tensor.matmul(T.ps[0:1, 0:256], T.ones[:, 0:1], T.xs[:], True, True).then_inc(sem.smm, 1)
+    g.tensor.wait_ge(sem.uin, 16)
+    g.tensor.matmul(T.py[:, 0:256], T.us[:], T.xs[:], True, m == 0).then_inc(sem.ymm, 1)
+    if m:
+        g.tensor.wait_ge(sem.rin, 16)
+        g.tensor.matmul(T.py[:, 0:256], T.ones[0:m, :], T.rows[0:m, :], False, True).then_inc(sem.ymm, 1)
+
+    if sends:
+        g.scalar.wait_ge(sem.scp, 1)
+        g.scalar.dma_start(T.mine[:], T.srow[0:1, :]).then_inc(sem.mined, 16)
+    if m:
+        if n_near:
+            g.scalar.wait_ge(sem.near, n_near)
+        if n_far:
+            g.scalar.wait_ge(sem.far, n_far)
+        g.scalar.dma_start(T.rows[0:m, :], T.slots[0:m]).then_inc(sem.rin, 16)
+
+    if sends:
+        g.wait_ge(sem.mined, 16)
+        left = 0
+        if am_relay:
+            out = [group[j] for j in range(k + 1, len(group))]
+            g.remote_dma_fused([transfer([T.mine[:]], grp, lambda d: 2 * k, engine(grp, i), sem.far)
+                                for i, grp in enumerate(out)], local_sem=sem.sent)
+            g.wait_ge(sem.near, n_near)
+            others = [T.slots[near_slot(rank, q)] for q in near_order(rank)]
+            g.remote_dma_fused([transfer(others, grp, lambda d: 2 * k + 1, engine(grp, i), sem.far)
+                                for i, grp in enumerate(out)], local_sem=sem.sent)
+            left = 2 * len(out)
+        else:
+            dsts = near_dsts(rank)
+            g.remote_dma_fused([transfer([T.mine[:]], dsts, lambda d: near_slot(d, rank), engine(dsts, 0), sem.near)],
+                               local_sem=sem.sent)
+            left = 1
+        g.wait_ge(sem.sent, left)
+
+    g.vector.wait_ge(sem.ymm, 2 if m else 1)
+    g.vector.tensor_copy(T.ys[:], T.py[:, 0:256]).then_inc(sem.ycp, 1)
+    g.sync.wait_ge(sem.ycp, 1)
+    g.sync.dma_start(T.y[:], T.ys[:]).then_inc(sem.yout, 16)
+    g.sync.wait_ge(sem.yout, 16)

@@ -1,10 +1,13 @@
 from concourse.bass import DstId, RemoteDMATransfer
 
+NEAR_ENGINES = 8
+
 SCRATCH = {
     "xs": ("sbuf", [128, 256], "bfloat16"),
     "us": ("sbuf", [128, 128], "bfloat16"),
     "ones": ("sbuf", [128, 128], "bfloat16"),
-    "srow": ("sbuf", [128, 256], "bfloat16"),
+    "st": ("sbuf", [128, 2], "bfloat16"),
+    "srow": ("sbuf", [128, 64], "bfloat16"),
     "rows": ("sbuf", [128, 256], "bfloat16"),
     "ys": ("sbuf", [128, 256], "bfloat16"),
     "mine": ("dram", [128, 2], "bfloat16"),
@@ -54,12 +57,12 @@ def rank_program(g, core, T, topo):
         first = [relay[k]] if relay[k] is not None and relay[k] != q else []
         return first + [d for d in group[k] if d > q and d not in first]
 
-    def engine(dsts, i):
+    def engines(dsts, i, count):
         m = topo.mask(core, cores[dsts[0]])
         for d in dsts:
             m &= topo.mask(core, cores[d])
         bits = [1 << b for b in range(m.bit_length()) if (m >> b) & 1]
-        return bits[i % len(bits)]
+        return sum(bits[(i + j) % len(bits)] for j in range(count))
 
     def transfer(srcs, dsts, slot_of, eng, rsem):
         ids = []
@@ -72,31 +75,36 @@ def rank_program(g, core, T, topo):
     k = kof[rank]
     m = 2 * k + len([r for r in group[k] if r < rank])
     am_relay = relay[k] == rank
-    sends = am_relay or len(near_dsts(rank)) > 0
-    n_near = len([q for q in group[k] if q != rank and rank in near_dsts(q)])
+    dsts = [] if am_relay else near_dsts(rank)
+    n_near = NEAR_ENGINES * len([q for q in group[k] if q != rank and rank in near_dsts(q)])
     n_far = 2 * k
 
     g.sync.dma_start(T.xs[:], T.x[:]).then_inc(sem.xin, 16)
     g.sync.dma_start(T.us[:], T.u[:]).then_inc(sem.uin, 16)
 
     g.vector.memset(T.ones[:], 1.0).then_inc(sem.ones, 1)
-    if sends:
-        g.vector.wait_ge(sem.smm, 1)
-        g.vector.tensor_copy(T.srow[0:1, :], T.ps[0:1, 0:256]).then_inc(sem.scp, 1)
-
     g.tensor.wait_ge(sem.ones, 1)
     g.tensor.wait_ge(sem.xin, 16)
-    if sends:
-        g.tensor.matmul(T.ps[0:1, 0:256], T.ones[:, 0:1], T.xs[:], True, True).then_inc(sem.smm, 1)
+    if am_relay:
+        for a in range(4):
+            g.tensor.matmul(T.ps[32 * a:32 * a + 32, 0:64], T.ones[:, 0:32], T.xs[:, 64 * a:64 * a + 64],
+                            True, True).then_inc(sem.smm, 1)
+        g.vector.wait_ge(sem.smm, 4)
+        g.vector.tensor_copy(T.srow[:], T.ps[:, 0:64]).then_inc(sem.scp, 1)
+    elif dsts:
+        for j in range(2):
+            g.tensor.matmul(T.ps[:, j:j + 1], T.xs[:, j::2], T.ones[:, 0:1], True, True).then_inc(sem.smm, 1)
+        g.vector.wait_ge(sem.smm, 2)
+        g.vector.tensor_copy(T.st[:], T.ps[:, 0:2]).then_inc(sem.scp, 1)
     g.tensor.wait_ge(sem.uin, 16)
     g.tensor.matmul(T.py[:, 0:256], T.us[:], T.xs[:], True, m == 0).then_inc(sem.ymm, 1)
     if m:
         g.tensor.wait_ge(sem.rin, 16)
         g.tensor.matmul(T.py[:, 0:256], T.ones[0:m, :], T.rows[0:m, :], False, True).then_inc(sem.ymm, 1)
 
-    if sends:
+    if am_relay:
         g.scalar.wait_ge(sem.scp, 1)
-        g.scalar.dma_start(T.mine[:], T.srow[0:1, :]).then_inc(sem.mined, 16)
+        g.scalar.dma_start(T.mine[:], T.srow[0:128:32, :]).then_inc(sem.mined, 16)
     if m:
         if n_near:
             g.scalar.wait_ge(sem.near, n_near)
@@ -104,24 +112,22 @@ def rank_program(g, core, T, topo):
             g.scalar.wait_ge(sem.far, n_far)
         g.scalar.dma_start(T.rows[0:m, :], T.slots[0:m]).then_inc(sem.rin, 16)
 
-    if sends:
+    if am_relay:
+        out = [group[j] for j in range(k + 1, len(group))]
         g.wait_ge(sem.mined, 16)
-        left = 0
-        if am_relay:
-            out = [group[j] for j in range(k + 1, len(group))]
-            g.remote_dma_fused([transfer([T.mine[:]], grp, lambda d: 2 * k, engine(grp, i), sem.far)
-                                for i, grp in enumerate(out)], local_sem=sem.sent)
-            g.wait_ge(sem.near, n_near)
-            others = [T.slots[near_slot(rank, q)] for q in near_order(rank)]
-            g.remote_dma_fused([transfer(others, grp, lambda d: 2 * k + 1, engine(grp, i), sem.far)
-                                for i, grp in enumerate(out)], local_sem=sem.sent)
-            left = 2 * len(out)
-        else:
-            dsts = near_dsts(rank)
-            g.remote_dma_fused([transfer([T.mine[:]], dsts, lambda d: near_slot(d, rank), engine(dsts, 0), sem.near)],
-                               local_sem=sem.sent)
-            left = 1
-        g.wait_ge(sem.sent, left)
+        g.remote_dma_fused([transfer([T.mine[:]], grp, lambda d: 2 * k, engines(grp, i, 1), sem.far)
+                            for i, grp in enumerate(out)], local_sem=sem.sent)
+        g.wait_ge(sem.near, n_near)
+        others = [T.slots[near_slot(rank, q)] for q in near_order(rank)]
+        g.remote_dma_fused([transfer(others, grp, lambda d: 2 * k + 1, engines(grp, i, 1), sem.far)
+                            for i, grp in enumerate(out)], local_sem=sem.sent)
+        g.wait_ge(sem.sent, 2 * len(out))
+    elif dsts:
+        g.wait_ge(sem.scp, 1)
+        for d in dsts:
+            g.remote_dma_fused([transfer([T.st[:]], [d], lambda e: near_slot(e, rank),
+                                         engines([d], 0, NEAR_ENGINES), sem.near)], local_sem=sem.sent)
+        g.wait_ge(sem.sent, NEAR_ENGINES * len(dsts))
 
     g.vector.wait_ge(sem.ymm, 2 if m else 1)
     g.vector.tensor_copy(T.ys[:], T.py[:, 0:256]).then_inc(sem.ycp, 1)

@@ -1,21 +1,26 @@
 from concourse.bass import DstId, RemoteDMATransfer
 
 NEAR_ENGINES = 8
+FOLD0 = 14
 
 SCRATCH = {
     "xs": ("sbuf", [128, 256], "bfloat16"),
     "us": ("sbuf", [128, 128], "bfloat16"),
     "ones": ("sbuf", [128, 128], "bfloat16"),
     "st": ("sbuf", [128, 2], "bfloat16"),
+    "st2": ("sbuf", [128, 2], "bfloat16"),
     "srow": ("sbuf", [128, 64], "bfloat16"),
     "rows": ("sbuf", [128, 256], "bfloat16"),
     "ys": ("sbuf", [128, 256], "bfloat16"),
+    "raw": ("dram", [128, 2], "bfloat16"),
     "mine": ("dram", [128, 2], "bfloat16"),
-    "slots": ("dram", [12, 128, 2], "bfloat16"),
+    "slots": ("dram", [16, 128, 2], "bfloat16"),
     "py": ("psum", [128, 512], "float32"),
     "ps": ("psum", [128, 512], "float32"),
+    "ps2": ("psum", [128, 512], "float32"),
 }
-SEMAPHORES = ["ones", "xin", "uin", "smm", "scp", "mined", "near", "far", "rin", "ymm", "ycp", "yout", "sent"]
+SEMAPHORES = ["ones", "xin", "uin", "rawd", "smm", "scp", "smm2", "scp2", "mined", "near", "fsem", "far", "rin",
+              "ymm", "ycp", "yout", "sent"]
 
 
 def rank_program(g, core, T, topo):
@@ -44,18 +49,16 @@ def rank_program(g, core, T, topo):
     for k, grp in enumerate(group):
         able = [r for r in grp if all(topo.may_write(cores[r], cores[d]) for d in later(k))]
         relay.append(able[-1] if later(k) else None)
+        assert relay[k] is None or relay[k] == grp[-1]
 
-    def near_order(d):
-        grp = group[kof[d]]
-        return [r for r in grp if r < d] + [r for r in grp if r > d]
+    def far_slot(j, t):
+        return 3 * j + t
 
-    def near_slot(d, q):
-        return 2 * kof[d] + near_order(d).index(q)
+    def near_slot(d, q, t):
+        return 3 * kof[d] + 2 * group[kof[d]].index(q) + t
 
-    def near_dsts(q):
-        k = kof[q]
-        first = [relay[k]] if relay[k] is not None and relay[k] != q else []
-        return first + [d for d in group[k] if d > q and d not in first]
+    def fold_slot(q):
+        return FOLD0 + group[kof[q]].index(q)
 
     def engines(dsts, i, count):
         m = topo.mask(core, cores[dsts[0]])
@@ -73,12 +76,19 @@ def rank_program(g, core, T, topo):
                                  dsts=[T.slots[slot_of(d)] for d in dsts], alu_op=1 if len(srcs) > 1 else 0)
 
     k = kof[rank]
-    m = 2 * k + len([r for r in group[k] if r < rank])
-    am_relay = relay[k] == rank
-    dsts = [] if am_relay else near_dsts(rank)
-    n_near = NEAR_ENGINES * len([q for q in group[k] if q != rank and rank in near_dsts(q)])
-    n_far = 2 * k
+    before = [q for q in group[k] if q < rank]
+    after = [d for d in group[k] if d > rank]
+    rel = relay[k]
+    am_relay = rel == rank
+    to_relay = rel is not None and not am_relay
+    m = 3 * k + 2 * len(before)
+    assert m <= FOLD0
+    n_near = 2 * NEAR_ENGINES * len(before)
+    n_far = 3 * k
+    last = 127
 
+    if am_relay or after:
+        g.scalar.dma_start(T.raw[:], T.x[last:last + 1, :]).then_inc(sem.rawd, 16)
     g.sync.dma_start(T.xs[:], T.x[:]).then_inc(sem.xin, 16)
     g.sync.dma_start(T.us[:], T.u[:]).then_inc(sem.uin, 16)
 
@@ -87,15 +97,20 @@ def rank_program(g, core, T, topo):
     g.tensor.wait_ge(sem.xin, 16)
     if am_relay:
         for a in range(4):
-            g.tensor.matmul(T.ps[32 * a:32 * a + 32, 0:64], T.ones[:, 0:32], T.xs[:, 64 * a:64 * a + 64],
+            g.tensor.matmul(T.ps[32 * a:32 * a + 32, 0:64], T.ones[0:last, 0:32], T.xs[0:last, 64 * a:64 * a + 64],
                             True, True).then_inc(sem.smm, 1)
         g.vector.wait_ge(sem.smm, 4)
         g.vector.tensor_copy(T.srow[:], T.ps[:, 0:64]).then_inc(sem.scp, 1)
-    elif dsts:
+    if to_relay:
         for j in range(2):
             g.tensor.matmul(T.ps[:, j:j + 1], T.xs[:, j::2], T.ones[:, 0:1], True, True).then_inc(sem.smm, 1)
         g.vector.wait_ge(sem.smm, 2)
         g.vector.tensor_copy(T.st[:], T.ps[:, 0:2]).then_inc(sem.scp, 1)
+    if after:
+        for j in range(2):
+            g.tensor.matmul(T.ps2[:, j:j + 1], T.xs[0:last, j::2], T.ones[0:last, 0:1], True, True).then_inc(sem.smm2, 1)
+        g.vector.wait_ge(sem.smm2, 2)
+        g.vector.tensor_copy(T.st2[:], T.ps2[:, 0:2]).then_inc(sem.scp2, 1)
     g.tensor.wait_ge(sem.uin, 16)
     g.tensor.matmul(T.py[:, 0:256], T.us[:], T.xs[:], True, m == 0).then_inc(sem.ymm, 1)
     if m:
@@ -114,20 +129,34 @@ def rank_program(g, core, T, topo):
 
     if am_relay:
         out = [group[j] for j in range(k + 1, len(group))]
+
+        def spread(srcs, t):
+            g.remote_dma_fused([transfer(srcs, grp, lambda d: far_slot(k, t), engines(grp, i, 1), sem.far)
+                                for i, grp in enumerate(out)], local_sem=sem.sent)
+
+        g.wait_ge(sem.rawd, 16)
+        spread([T.raw[:]], 0)
         g.wait_ge(sem.mined, 16)
-        g.remote_dma_fused([transfer([T.mine[:]], grp, lambda d: 2 * k, engines(grp, i, 1), sem.far)
-                            for i, grp in enumerate(out)], local_sem=sem.sent)
-        g.wait_ge(sem.near, n_near)
-        others = [T.slots[near_slot(rank, q)] for q in near_order(rank)]
-        g.remote_dma_fused([transfer(others, grp, lambda d: 2 * k + 1, engines(grp, i, 1), sem.far)
-                            for i, grp in enumerate(out)], local_sem=sem.sent)
-        g.wait_ge(sem.sent, 2 * len(out))
-    elif dsts:
-        g.wait_ge(sem.scp, 1)
-        for d in dsts:
-            g.remote_dma_fused([transfer([T.st[:]], [d], lambda e: near_slot(e, rank),
-                                         engines([d], 0, NEAR_ENGINES), sem.near)], local_sem=sem.sent)
-        g.wait_ge(sem.sent, NEAR_ENGINES * len(dsts))
+        spread([T.mine[:]], 1)
+        g.wait_ge(sem.fsem, NEAR_ENGINES * len(before))
+        spread([T.slots[fold_slot(q)] for q in before], 2)
+        g.wait_ge(sem.sent, 3 * len(out))
+    elif after:
+        calls = 0
+        g.wait_ge(sem.rawd, 16)
+        g.remote_dma_fused([transfer([T.raw[:]], after, lambda d: near_slot(d, rank, 0),
+                                     engines(after, 0, NEAR_ENGINES), sem.near)], local_sem=sem.sent)
+        calls += 1
+        if to_relay:
+            g.wait_ge(sem.scp, 1)
+            g.remote_dma_fused([transfer([T.st[:]], [rel], lambda d: fold_slot(rank),
+                                         engines([rel], 0, NEAR_ENGINES), sem.fsem)], local_sem=sem.sent)
+            calls += 1
+        g.wait_ge(sem.scp2, 1)
+        g.remote_dma_fused([transfer([T.st2[:]], after, lambda d: near_slot(d, rank, 1),
+                                     engines(after, 0, NEAR_ENGINES), sem.near)], local_sem=sem.sent)
+        calls += 1
+        g.wait_ge(sem.sent, NEAR_ENGINES * calls)
 
     g.vector.wait_ge(sem.ymm, 2 if m else 1)
     g.vector.tensor_copy(T.ys[:], T.py[:, 0:256]).then_inc(sem.ycp, 1)

from concourse.bass import DstId, RemoteDMATransfer

NEAR_ENGINES = 8
FOLD0 = 14

SCRATCH = {
    "xs": ("sbuf", [128, 256], "bfloat16"),
    "us": ("sbuf", [128, 128], "bfloat16"),
    "ones": ("sbuf", [128, 128], "bfloat16"),
    "st": ("sbuf", [128, 2], "bfloat16"),
    "st2": ("sbuf", [128, 2], "bfloat16"),
    "srow": ("sbuf", [128, 64], "bfloat16"),
    "rows": ("sbuf", [128, 256], "bfloat16"),
    "ys": ("sbuf", [128, 256], "bfloat16"),
    "raw": ("dram", [128, 2], "bfloat16"),
    "mine": ("dram", [128, 2], "bfloat16"),
    "slots": ("dram", [16, 128, 2], "bfloat16"),
    "py": ("psum", [128, 512], "float32"),
    "ps": ("psum", [128, 512], "float32"),
    "ps2": ("psum", [128, 512], "float32"),
}
SEMAPHORES = ["ones", "xin", "uin", "rawd", "smm", "scp", "smm2", "scp2", "mined", "near", "fsem", "far", "rin",
              "ymm", "ycp", "yout", "sent"]


def rank_program(g, core, T, topo):
    rank = T.rank_of(core)
    if rank is None:
        return
    sem = T.sem
    cores = list(T.cores)
    n = len(cores)

    chips = []
    for c in cores:
        if topo.chip(c) not in chips:
            chips.append(topo.chip(c))
    group = [[r for r in range(n) if topo.chip(cores[r]) == ch] for ch in chips]
    kof = {}
    for k, grp in enumerate(group):
        assert grp == list(range(grp[0], grp[0] + len(grp)))
        for r in grp:
            kof[r] = k

    def later(k):
        return [r for grp in group[k + 1:] for r in grp]

    relay = []
    for k, grp in enumerate(group):
        able = [r for r in grp if all(topo.may_write(cores[r], cores[d]) for d in later(k))]
        relay.append(able[-1] if later(k) else None)
        assert relay[k] is None or relay[k] == grp[-1]

    def far_slot(j, t):
        return 3 * j + t

    def near_slot(d, q, t):
        return 3 * kof[d] + 2 * group[kof[d]].index(q) + t

    def fold_slot(q):
        return FOLD0 + group[kof[q]].index(q)

    def engines(dsts, i, count):
        m = topo.mask(core, cores[dsts[0]])
        for d in dsts:
            m &= topo.mask(core, cores[d])
        bits = [1 << b for b in range(m.bit_length()) if (m >> b) & 1]
        return sum(bits[(i + j) % len(bits)] for j in range(count))

    def transfer(srcs, dsts, slot_of, eng, rsem):
        ids = []
        for d in dsts:
            rid, pid, _se = topo.addr(cores[d])
            ids.append(DstId(rid=rid, pnc=pid))
        return RemoteDMATransfer(dst_ids=ids, dma_engine_mask=eng, remote_sem=rsem, srcs=srcs,
                                 dsts=[T.slots[slot_of(d)] for d in dsts], alu_op=1 if len(srcs) > 1 else 0)

    k = kof[rank]
    before = [q for q in group[k] if q < rank]
    after = [d for d in group[k] if d > rank]
    rel = relay[k]
    am_relay = rel == rank
    to_relay = rel is not None and not am_relay
    m = 3 * k + 2 * len(before)
    assert m <= FOLD0
    n_near = 2 * NEAR_ENGINES * len(before)
    n_far = 3 * k
    last = 127

    if am_relay or after:
        g.scalar.dma_start(T.raw[:], T.x[last:last + 1, :]).then_inc(sem.rawd, 16)
    g.sync.dma_start(T.xs[:], T.x[:]).then_inc(sem.xin, 16)
    g.sync.dma_start(T.us[:], T.u[:]).then_inc(sem.uin, 16)

    g.vector.memset(T.ones[:], 1.0).then_inc(sem.ones, 1)
    g.tensor.wait_ge(sem.ones, 1)
    g.tensor.wait_ge(sem.xin, 16)
    if am_relay:
        for a in range(4):
            g.tensor.matmul(T.ps[32 * a:32 * a + 32, 0:64], T.ones[0:last, 0:32], T.xs[0:last, 64 * a:64 * a + 64],
                            True, True).then_inc(sem.smm, 1)
        g.vector.wait_ge(sem.smm, 4)
        g.vector.tensor_copy(T.srow[:], T.ps[:, 0:64]).then_inc(sem.scp, 1)
    if to_relay:
        for j in range(2):
            g.tensor.matmul(T.ps[:, j:j + 1], T.xs[:, j::2], T.ones[:, 0:1], True, True).then_inc(sem.smm, 1)
        g.vector.wait_ge(sem.smm, 2)
        g.vector.tensor_copy(T.st[:], T.ps[:, 0:2]).then_inc(sem.scp, 1)
    if after:
        for j in range(2):
            g.tensor.matmul(T.ps2[:, j:j + 1], T.xs[0:last, j::2], T.ones[0:last, 0:1], True, True).then_inc(sem.smm2, 1)
        g.vector.wait_ge(sem.smm2, 2)
        g.vector.tensor_copy(T.st2[:], T.ps2[:, 0:2]).then_inc(sem.scp2, 1)
    g.tensor.wait_ge(sem.uin, 16)
    g.tensor.matmul(T.py[:, 0:256], T.us[:], T.xs[:], True, m == 0).then_inc(sem.ymm, 1)
    if m:
        g.tensor.wait_ge(sem.rin, 16)
        g.tensor.matmul(T.py[:, 0:256], T.ones[0:m, :], T.rows[0:m, :], False, True).then_inc(sem.ymm, 1)

    if am_relay:
        g.scalar.wait_ge(sem.scp, 1)
        g.scalar.dma_start(T.mine[:], T.srow[0:128:32, :]).then_inc(sem.mined, 16)
    if m:
        if n_near:
            g.scalar.wait_ge(sem.near, n_near)
        if n_far:
            g.scalar.wait_ge(sem.far, n_far)
        g.scalar.dma_start(T.rows[0:m, :], T.slots[0:m]).then_inc(sem.rin, 16)

    if am_relay:
        out = [group[j] for j in range(k + 1, len(group))]

        def spread(srcs, t):
            g.remote_dma_fused([transfer(srcs, grp, lambda d: far_slot(k, t), engines(grp, i, 1), sem.far)
                                for i, grp in enumerate(out)], local_sem=sem.sent)

        g.wait_ge(sem.rawd, 16)
        spread([T.raw[:]], 0)
        g.wait_ge(sem.mined, 16)
        spread([T.mine[:]], 1)
        g.wait_ge(sem.fsem, NEAR_ENGINES * len(before))
        spread([T.slots[fold_slot(q)] for q in before], 2)
        g.wait_ge(sem.sent, 3 * len(out))
    elif after:
        calls = 0
        g.wait_ge(sem.rawd, 16)
        g.remote_dma_fused([transfer([T.raw[:]], after, lambda d: near_slot(d, rank, 0),
                                     engines(after, 0, NEAR_ENGINES), sem.near)], local_sem=sem.sent)
        calls += 1
        if to_relay:
            g.wait_ge(sem.scp, 1)
            g.remote_dma_fused([transfer([T.st[:]], [rel], lambda d: fold_slot(rank),
                                         engines([rel], 0, NEAR_ENGINES), sem.fsem)], local_sem=sem.sent)
            calls += 1
        g.wait_ge(sem.scp2, 1)
        g.remote_dma_fused([transfer([T.st2[:]], after, lambda d: near_slot(d, rank, 1),
                                     engines(after, 0, NEAR_ENGINES), sem.near)], local_sem=sem.sent)
        calls += 1
        g.wait_ge(sem.sent, NEAR_ENGINES * calls)

    g.vector.wait_ge(sem.ymm, 2 if m else 1)
    g.vector.tensor_copy(T.ys[:], T.py[:, 0:256]).then_inc(sem.ycp, 1)
    g.sync.wait_ge(sem.ycp, 1)
    g.sync.dma_start(T.y[:], T.ys[:]).then_inc(sem.yout, 16)
    g.sync.wait_ge(sem.yout, 16)
